import numpy as np
import ml_dtypes


def mxq(x, axis, fmt="e4m3"):
    dtype, down = {"e4m3": (ml_dtypes.float8_e4m3fn, 7), "e5m2": (ml_dtypes.float8_e5m2, 14)}[fmt]
    v = np.moveaxis(np.asarray(x, np.float32).astype(ml_dtypes.bfloat16).astype(np.float64), axis, -1)
    blocks = v.reshape(v.shape[:-1] + (-1, 32))
    amax = np.abs(blocks).max(-1, keepdims=True)
    byte = np.maximum(np.where(amax > 0, np.frexp(amax)[1] - 1 + 127, 0) - down, 1)
    scale = np.exp2(byte - 127.0)
    codes = (blocks / scale).astype(np.float32).astype(dtype).astype(np.float64)
    return np.moveaxis((codes * scale).reshape(v.shape), -1, axis)


WIDE = False


def mx_kscale(k):
    if not WIDE:
        return np.ones(k)
    levels = np.array([10, -10, 5, -5, 0])
    if k % 512:
        return np.exp2(np.random.permutation(np.resize(levels, k // 32))).repeat(32)
    a = np.empty((k // 512, 16))
    for p in range(k // 512):
        a[p, :8] = np.random.permutation(np.resize(levels, 8))
        for g in range(8):
            far = levels[np.abs(levels - a[p, g]) >= 10]
            a[p, g + 8] = far[np.random.randint(len(far))]
    return np.exp2(a.ravel()).repeat(32)


BF16 = ml_dtypes.bfloat16


def bf(x):
    return np.asarray(x, np.float32).astype(BF16)


def f64(x):
    return np.asarray(x).astype(np.float64)


E2M1 = np.array([0.0, 0.5, 1.0, 1.5, 2.0, 3.0, 4.0, 6.0, -0.0, -0.5, -1.0, -1.5, -2.0, -3.0, -4.0, -6.0])


def pack_weight(w, fmt):
    k, n = w.shape
    w = f64(bf(w)).reshape(k // 32, 32, n)
    amax = np.abs(w).max(1)
    if fmt == "e4m3":
        byte = np.frexp(amax)[1] - 1 + 127 - 7
    else:
        mant, ex = np.frexp(amax / 6.0)
        byte = np.where(mant > 0.5, ex, ex - 1) + 127
    byte = np.clip(np.where(amax > 0, byte, 1), 1, 254)
    scaled = (w * np.exp2(127.0 - byte)[:, None, :]).reshape(k, n).astype(np.float32)
    by_word = np.ascontiguousarray(scaled.reshape(k // 512, 128, 4, n).transpose(0, 1, 3, 2))
    if fmt == "e4m3":
        words = by_word.astype(ml_dtypes.float8_e4m3fn).view(np.uint8)
    else:
        c = by_word.astype(ml_dtypes.float4_e2m1fn).view(np.uint8) & 0xF
        words = c[..., 0::2] | (c[..., 1::2] << 4)
    return np.ascontiguousarray(words), np.ascontiguousarray(byte.astype(np.uint8).reshape(k // 512, 16, n))


def unpack_weight(words, scales, fmt):
    g, p, n, _ = words.shape
    if fmt == "e4m3":
        vals = np.ascontiguousarray(words).view(ml_dtypes.float8_e4m3fn).astype(np.float64)
    else:
        nib = np.empty((g, p, n, 4), np.uint8)
        nib[..., 0::2] = words & 0xF
        nib[..., 1::2] = words >> 4
        vals = E2M1[nib]
    vals = vals * np.repeat(np.exp2(scales.astype(np.float64) - 127.0), 8, axis=1)[..., None]
    return vals.transpose(0, 1, 3, 2).reshape(g * 512, n)
def pack4(w):
    words, scales = pack_weight(w, "e2m1")
    return words.reshape(words.shape[0], 128, -1), scales


def unpack4(words, scales):
    return unpack_weight(words.reshape(words.shape[0], 128, -1, 2), scales, "e2m1")


T, M, L, F = 2048, 1024, 512, 1024


def setup_inputs():
    s = mx_kscale(M)
    t = mx_kscale(L)
    codes = np.random.standard_normal((M, T)) * s[:, None]
    book = np.random.standard_normal((M, L)) / np.sqrt(M) / s[:, None] * t
    omega = np.pi * (np.arange(F) + np.random.random_sample(F)) / F
    angle = (np.arange(L)[:, None] + 0.5) * omega
    trig = np.concatenate([np.cos(angle), np.sin(angle)], axis=1) * np.sqrt(2 / L) / t[:, None]
    code_words, code_scales = pack4(codes)
    book_words, book_scales = pack4(book)
    trig_words, trig_scales = pack_weight(trig, "e4m3")
    return {"code_words": code_words, "code_scales": code_scales,
            "book_words": book_words, "book_scales": book_scales,
            "mean": bf(0.3 * np.random.standard_normal(L) * t),
            "trig_words": trig_words, "trig_scales": trig_scales,
            "noise": bf(np.random.uniform(0.5, 1.0, F))}


def reference(code_words, code_scales, book_words, book_scales, mean, trig_words, trig_scales, noise):
    codes = unpack4(code_words, code_scales)
    book = unpack4(book_words, book_scales)
    trig = unpack_weight(trig_words, trig_scales, "e4m3")
    a = (codes.T @ book) + f64(mean)
    z = mxq(a, 1, "e4m3") @ trig
    z2 = np.square(z)
    power = z2[:, :F] + z2[:, F:] + f64(noise)
    env = 1.0 / power
    return env, np.log(env)

@@ -1,0 +1,337 @@
+from contextlib import ExitStack
+
+import concourse.mybir as mybir
+from concourse.masks import make_identity
+
+T, M, L, F = 2048, 1024, 512, 1024
+P = 128
+FLOPS = 2 * T * M * L + 2 * T * L * 2 * F + 6 * T * F
+F32 = mybir.dt.float32
+BF16 = mybir.dt.bfloat16
+I32 = mybir.dt.int32
+U32 = mybir.dt.uint32
+U8 = mybir.dt.uint8
+FP4X4 = mybir.dt.float4_e2m1fn_x4
+FP8X4 = mybir.dt.float8_e4m3fn_x4
+ACT = mybir.ActivationFunctionType
+ALU = mybir.AluOpType
+AX = mybir.AxisListType
+
+G = M // 512
+TB = 512
+CELLS = (T // TB) * (F // P)
+PHASES = ((0, "L"), (22, "E"))
+VEC_Y = {"L": 0.4, "E": 1.0}
+VEC_X = {"L": 0.0, "E": 0.5}
+ACCUM = {"L": 0.5, "E": 1.0}
+TURNS = 2
+LOGS = 2
+LAG = 6
+YB, PB = 18, 18
+
+
+def tile_floored_inverse_filter_envelope_s4_kernel(
+    tc, code_words, code_scales, book_words, book_scales, mean, trig_words, trig_scales, noise, env_out, log_out
+):
+    nc = tc.nc
+    with ExitStack() as ctx:
+        const = ctx.enter_context(tc.tile_pool(name="const", bufs=1))
+        work = ctx.enter_context(tc.tile_pool(name="work", bufs=3))
+        psum = ctx.enter_context(tc.psum_pool(name="psum", bufs=2))
+        ctx.enter_context(tc.manual_schedule())
+
+        book_plane = const.tile([P, G, L], U8, name="book_plane", align_bytes=64)
+        code_plane = const.tile([P, G, T], U8, name="code_plane", align_bytes=64)
+        trig_plane = const.tile([P, 1, 2 * F], U8, name="trig_plane", align_bytes=64)
+        for plane in (book_plane, code_plane, trig_plane):
+            nc.vector.memset(plane[:].rearrange("p g n -> p (g n)").bitcast(I32), 0)
+        book_raw = const.tile([P, G, 2 * L], U8, name="book_raw", align_bytes=64)
+        nc.sync.dma_start(out=book_raw[:].bitcast(I32), in_=book_words.bitcast(I32).rearrange("g p n -> p g n"))
+        code_tiles = []
+        for b in range(T // TB):
+            code_tiles.append(const.tile([P, G, 2 * TB], U8, name="codes%d" % b, align_bytes=64))
+        cw = code_words.bitcast(I32).rearrange("g p n -> p g n")
+        w32 = 2 * TB // 4
+
+        def load_codes(b):
+            nc.sync.dma_start(out=code_tiles[b][:].bitcast(I32), in_=cw[:, :, b * w32 : (b + 1) * w32])
+
+        trig = {}
+        tw = trig_words.rearrange("g p n t -> p (g n t)").bitcast(I32)
+        for part in (0, 1):
+            for h in (0, 1):
+                trig[part, h] = const.tile([P, 512], I32, name="trig%d%d" % (part, h), align_bytes=64)
+
+        def load_trig(part, h):
+            n0 = part * F + h * 512
+            nc.sync.dma_start(out=trig[part, h][:], in_=tw[:, n0 : n0 + 512])
+
+        def load_scales(queue, plane, source, q):
+            queue.dma_start(
+                out=plane[:].bitcast(I32)[32 * q : 32 * q + 4],
+                in_=source.bitcast(I32)[:, 4 * q : 4 * q + 4, :].rearrange("g r n -> r g n"),
+            )
+
+        for q in range(4):
+            load_scales(nc.scalar, book_plane, book_scales, q)
+        load_codes(0)
+        load_scales(nc.scalar, code_plane, code_scales, 0)
+        load_scales(nc.scalar, code_plane, code_scales, 1)
+        load_scales(nc.gpsimd, code_plane, code_scales, 2)
+        load_scales(nc.gpsimd, code_plane, code_scales, 3)
+        mean_col = const.tile([P, 4], BF16, name="mean_col")
+        nc.sync.dma_start(out=mean_col[:], in_=mean.rearrange("(p j) -> p j", j=4))
+        for q in range(4):
+            load_scales(nc.sync, trig_plane, trig_scales, q)
+        load_trig(0, 0)
+        load_trig(1, 0)
+        noise_bf = const.tile([P, F // P], BF16, name="noise_bf")
+        with nc.allow_non_contiguous_dma(reason="one noise value of each 128-frequency tile a partition"):
+            nc.sync.dma_start(out=noise_bf[:], in_=noise.rearrange("(i p) -> p i", p=P))
+        load_codes(1)
+        load_trig(0, 1)
+        load_trig(1, 1)
+        load_codes(2)
+        load_codes(3)
+
+        one = const.tile([P, 1], F32, name="one")
+        nc.gpsimd.memset(one[:], 1.0)
+        warm = const.tile([P, 1], F32, name="warm")
+        nc.scalar.activation(out=warm[:], in_=one[:], func=ACT.Ln)
+        ident = const.tile([P, P], F32, name="ident")
+        make_identity(nc, ident[:])
+
+        book_codes = const.tile([P, G, 4, 2 * P], U8, name="book_codes", align_bytes=64)
+        book_pp = const.tile([P, G, 4, P], U8, name="book_pp", align_bytes=64)
+        for g in range(G):
+            nc.vector.tensor_copy(
+                out=book_codes[:, g].rearrange("p j (m b) -> p j m b", b=2),
+                in_=book_raw[:, g].rearrange("p (m j b) -> p j m b", j=4, b=2),
+            )
+        nc.vector.tensor_copy(out=book_pp[:], in_=book_plane[:].rearrange("p g (m j) -> p g j m", j=4))
+        noise_col = const.tile([P, F // P], F32, name="noise_col")
+
+        a_ps, a_bf, a_codes, a_scales, zx, zy, xsq, ysq, power, pt, logp = ({} for _ in range(11))
+
+        def stage1_mm(s):
+            b, r = divmod(s, 4)
+            a_ps[s] = psum.tile([P, 4, P], F32, name="a_ps", tag="turn", bufs=4)
+            for j in range(4):
+                for g in range(G):
+                    nc.tensor.matmul_mx(
+                        out=a_ps[s][:, j, :],
+                        lhsT=book_codes[:, g, j, :].bitcast(FP4X4),
+                        lhsT_scale=book_pp[:, g, j, :],
+                        rhs=code_tiles[b][:, g, 2 * P * r : 2 * P * (r + 1)].bitcast(FP4X4),
+                        rhs_scale=code_plane[:, g, s * P : (s + 1) * P],
+                        start=(g == 0),
+                        stop=(g == G - 1),
+                    )
+
+        def add_mean(s):
+            a_bf[s] = work.tile([P, P, 4], BF16, name="a_bf", align_bytes=64)
+            nc.vector.tensor_tensor(
+                out=a_bf[s][:],
+                in0=a_ps[s][:].rearrange("p j n -> p n j"),
+                in1=mean_col[:].unsqueeze(1).to_broadcast([P, P, 4]),
+                op=ALU.add,
+            )
+
+        def quantise(s):
+            b, r = divmod(s, 4)
+            if r == 0:
+                a_codes[b] = work.tile([P, TB], U32, name="a_codes", align_bytes=64, bufs=2)
+                a_scales[b] = work.tile([P, TB], U8, name="a_scales", align_bytes=64, bufs=2)
+            cols = slice(r * P, (r + 1) * P)
+            nc.vector.quantize_mx(
+                out=a_codes[b][:, cols].bitcast(FP8X4),
+                scales=a_scales[b][:, cols],
+                in_=a_bf[s][:].rearrange("p n j -> p (n j)"),
+            )
+
+        def z_mm(c):
+            b, i = divmod(c, 8)
+            h, k = divmod(i, 4)
+            zx[c] = psum.tile([P, TB], F32, name="zx")
+            zy[c] = psum.tile([P, TB], F32, name="zy")
+            for part, z in ((0, zx[c]), (1, zy[c])):
+                nc.tensor.matmul_mx(
+                    out=z[:],
+                    lhsT=trig[part, h][:, k * P : (k + 1) * P].bitcast(FP8X4),
+                    lhsT_scale=trig_plane[:, 0, part * F + i * P : part * F + (i + 1) * P],
+                    rhs=a_codes[b][:].bitcast(FP8X4),
+                    rhs_scale=a_scales[b][:],
+                    start=True,
+                    stop=True,
+                )
+
+        def phase_of(c):
+            return [k for c0, k in PHASES if c0 <= c][-1]
+
+        def share(fractions):
+            chosen, acc = set(), 0.0
+            for c in range(CELLS):
+                acc += fractions[phase_of(c)]
+                if acc >= 0.999:
+                    chosen.add(c)
+                    acc -= 1.0
+            return chosen
+
+        vec_x, vec_y, accum = share(VEC_X), share(VEC_Y), share(ACCUM)
+
+        def square_scalar(c):
+            if c not in vec_x:
+                xsq[c] = work.tile([P, TB], F32, name="xsq")
+                nc.scalar.activation(out=xsq[c][:], in_=zx[c][:], func=ACT.Square)
+            if c not in vec_y:
+                ysq[c] = work.tile([P, TB], F32, name="ysq", bufs=YB)
+                nc.scalar.activation(out=ysq[c][:], in_=zy[c][:], func=ACT.Square)
+
+        def square_vector(c):
+            for chosen, z, sq, tag in ((vec_x, zx, xsq, "xsq"), (vec_y, zy, ysq, "ysq")):
+                if c in chosen:
+                    sq[c] = work.tile([P, TB], F32, name=tag, bufs=YB if tag == "ysq" else 3)
+                    nc.vector.tensor_reduce(
+                        out=sq[c][:],
+                        in_=z[c][:].unsqueeze(2).to_broadcast([P, TB, 2]),
+                        axis=AX.X,
+                        op=ALU.mult,
+                    )
+
+        def add_noise(c):
+            i = c % 8
+            power[c] = work.tile([P, TB], F32, name="power", bufs=PB)
+            if c in accum:
+                nc.gpsimd.tensor_scalar(
+                    out=power[c][:],
+                    in0=xsq[c][:],
+                    scalar1=1.0,
+                    scalar2=noise_col[:, i : i + 1],
+                    op0=ALU.mult,
+                    op1=ALU.add,
+                )
+            else:
+                nc.vector.scalar_tensor_tensor(
+                    out=power[c][:],
+                    in0=xsq[c][:],
+                    scalar=noise_col[:, i : i + 1],
+                    in1=ysq[c][:],
+                    op0=ALU.add,
+                    op1=ALU.add,
+                )
+
+        def transpose(q):
+            u, r = divmod(q, 4)
+            pt[u, r] = psum.tile([P, 4, P], F32, name="pt", tag="turn", bufs=4)
+            for k in range(4):
+                c = 4 * u + k
+                parts = (power[c], ysq[c]) if c in accum else (power[c],)
+                for n, part in enumerate(parts):
+                    nc.tensor.matmul(
+                        out=pt[u, r][:, k, :],
+                        lhsT=part[:, r * P : (r + 1) * P],
+                        rhs=ident[:],
+                        start=(n == 0),
+                        stop=(n == len(parts) - 1),
+                        is_transpose=True,
+                    )
+
+        def take_log(u, r):
+            b, h = divmod(u, 2)
+            t = 4 * b + r
+            if t not in logp:
+                logp[t] = work.tile([P, F], F32, name="logp", bufs=10)
+            nc.scalar.activation(
+                out=logp[t][:, h * 512 : (h + 1) * 512],
+                in_=pt[u, r][:].rearrange("p k f -> p (k f)"),
+                func=ACT.Ln,
+            )
+            if h == 1:
+                neg = work.tile([P, F], F32, name="neg")
+                nc.gpsimd.tensor_scalar(
+                    out=neg[:], in0=logp[t][:], scalar1=-1.0, scalar2=0.0, op0=ALU.mult, op1=ALU.add
+                )
+                nc.sync.dma_start(out=log_out[t * P : (t + 1) * P, :], in_=neg[:])
+
+        def take_exp(t):
+            env = work.tile([P, F], F32, name="env", bufs=4)
+            nc.scalar.activation(out=env[:], in_=logp[t][:], func=ACT.Exp, scale=-1.0)
+            nc.sync.dma_start(out=env_out[t * P : (t + 1) * P, :], in_=env[:])
+
+        for s in range(4):
+            stage1_mm(s)
+            add_mean(s)
+            if s > 0:
+                quantise(s - 1)
+        quantise(3)
+        nc.vector.tensor_copy(out=noise_col[:], in_=noise_bf[:])
+        z_mm(0)
+
+        turned = []
+        q_next = 0
+        logged, exped = set(), set()
+
+        def log_one():
+            q = turned.pop(0)
+            take_log(q // 4, q % 4)
+            logged.add(q)
+
+        def exp_one(t):
+            take_exp(t)
+            exped.add(t)
+
+        def ready_tiles():
+            return [t for t in range(16) if t not in exped and {8 * (t // 4) + t % 4, 8 * (t // 4) + 4 + t % 4} <= logged]
+
+        last_phase = "L"
+        exps = []
+        for c in range(CELLS):
+            b, i = divmod(c, 8)
+            phase = phase_of(c)
+            end = [c0 for c0, k in PHASES if c0 > c] + [CELLS]
+            if phase == "E" and last_phase == "L":
+                exps = ready_tiles()
+            last_phase = phase
+            if c + 1 < CELLS:
+                z_mm(c + 1)
+            s = 4 * (b + 1) + {0: 0, 1: 1, 3: 2, 4: 3}.get(i, 99)
+            if s < 16:
+                stage1_mm(s)
+            square_scalar(c)
+            if c > 0:
+                add_noise(c - 1)
+            square_vector(c)
+            s1 = 4 * (b + 1) + {1: 0, 2: 1, 4: 2, 5: 3}.get(i, 99)
+            if s1 < 16:
+                add_mean(s1)
+            s2 = 4 * (b + 1) + {2: 0, 3: 1, 5: 2, 6: 3}.get(i, 99)
+            if s2 < 16:
+                quantise(s2)
+            if phase == "L":
+                n = min(len(turned), LOGS)
+                for _ in range(n):
+                    log_one()
+            else:
+                n = -(-len(exps) // (end[0] - c))
+                for _ in range(n):
+                    exp_one(exps.pop(0))
+            ready_q = 4 * (((c - LAG) // 4) + 1) if c >= LAG else 0
+            n = 0
+            while n < max(TURNS, 1 if phase == "E" else (ready_q - q_next + 3) // 4) and len(turned) < 2 and q_next < ready_q:
+                transpose(q_next)
+                turned.append(q_next)
+                q_next += 1
+                n += 1
+        add_noise(CELLS - 1)
+        while turned:
+            log_one()
+        rest = [8 * b + 4 * h + r for b in range(4) for r in range(4) for h in (0, 1)]
+        rest = [q for q in rest if q not in logged]
+        for n in range(len(rest) + 1):
+            if n < len(rest):
+                transpose(rest[n])
+                turned.append(rest[n])
+            if n > 0:
+                log_one()
+        for t in ready_tiles():
+            exp_one(t)

@@ -20,14 +20,25 @@ AX = mybir.AxisListType
 G = M // 512
 TB = 512
 CELLS = (T // TB) * (F // P)
-PHASES = ((0, "L"), (22, "E"))
-VEC_Y = {"L": 0.4, "E": 1.0}
-VEC_X = {"L": 0.0, "E": 0.5}
-ACCUM = {"L": 0.5, "E": 1.0}
+PHASES = ((0, "L"),)
+VEC_Y = {"L": (0, 1, 3, 6), "E": ()}
+GPS_Y = {"L": (), "E": ()}
+VEC_X = {"L": (), "E": ()}
+ACCUM = {"L": (0, 2), "E": ()}
 TURNS = 2
 LOGS = 2
-LAG = 6
-YB, PB = 18, 18
+LAG = 5
+RECIP = 0
+TAILNEG = 1
+PLANE_V = 4
+HALVED = 2
+S1 = (0, 2, 3, 4)
+DLY = (1, 2)
+YB = 18
+PB = 10
+LB = 32
+EB = 8
+NB = 6
 
 
 def tile_floored_inverse_filter_envelope_s4_kernel(
@@ -101,14 +112,16 @@ def tile_floored_inverse_filter_envelope_s4_kernel(
         ident = const.tile([P, P], F32, name="ident")
         make_identity(nc, ident[:])
 
-        book_codes = const.tile([P, G, 4, 2 * P], U8, name="book_codes", align_bytes=64)
-        book_pp = const.tile([P, G, 4, P], U8, name="book_pp", align_bytes=64)
-        for g in range(G):
+        book_codes = [const.tile([P, G, 2 * P], U8, name="book_codes%d" % j, align_bytes=64) for j in range(4)]
+        book_pp = [const.tile([P, G, P], U8, name="book_pp%d" % j, align_bytes=64) for j in range(4)]
+        raw_by_slot = book_raw[:].rearrange("p g (m j b) -> p g j m b", j=4, b=2)
+        plane_by_slot = book_plane[:].rearrange("p g (m j) -> p g j m", j=4)
+        for j in range(4):
             nc.vector.tensor_copy(
-                out=book_codes[:, g].rearrange("p j (m b) -> p j m b", b=2),
-                in_=book_raw[:, g].rearrange("p (m j b) -> p j m b", j=4, b=2),
+                out=book_codes[j][:].rearrange("p g (m b) -> p g m b", b=2), in_=raw_by_slot[:, :, j]
             )
-        nc.vector.tensor_copy(out=book_pp[:], in_=book_plane[:].rearrange("p g (m j) -> p g j m", j=4))
+            engine = nc.vector if j < PLANE_V else nc.gpsimd
+            engine.tensor_copy(out=book_pp[j][:], in_=plane_by_slot[:, :, j])
         noise_col = const.tile([P, F // P], F32, name="noise_col")
 
         a_ps, a_bf, a_codes, a_scales, zx, zy, xsq, ysq, power, pt, logp = ({} for _ in range(11))
@@ -120,8 +133,8 @@ def tile_floored_inverse_filter_envelope_s4_kernel(
                 for g in range(G):
                     nc.tensor.matmul_mx(
                         out=a_ps[s][:, j, :],
-                        lhsT=book_codes[:, g, j, :].bitcast(FP4X4),
-                        lhsT_scale=book_pp[:, g, j, :],
+                        lhsT=book_codes[j][:, g, :].bitcast(FP4X4),
+                        lhsT_scale=book_pp[j][:, g, :],
                         rhs=code_tiles[b][:, g, 2 * P * r : 2 * P * (r + 1)].bitcast(FP4X4),
                         rhs_scale=code_plane[:, g, s * P : (s + 1) * P],
                         start=(g == 0),
@@ -152,8 +165,8 @@ def tile_floored_inverse_filter_envelope_s4_kernel(
         def z_mm(c):
             b, i = divmod(c, 8)
             h, k = divmod(i, 4)
-            zx[c] = psum.tile([P, TB], F32, name="zx")
-            zy[c] = psum.tile([P, TB], F32, name="zy")
+            zx[c] = psum.tile([P, TB], F32, name="zx", tag="zx", bufs=2)
+            zy[c] = psum.tile([P, TB], F32, name="zy", tag="zy", bufs=2)
             for part, z in ((0, zx[c]), (1, zy[c])):
                 nc.tensor.matmul_mx(
                     out=z[:],
@@ -168,22 +181,47 @@ def tile_floored_inverse_filter_envelope_s4_kernel(
         def phase_of(c):
             return [k for c0, k in PHASES if c0 <= c][-1]
 
-        def share(fractions):
-            chosen, acc = set(), 0.0
-            for c in range(CELLS):
-                acc += fractions[phase_of(c)]
-                if acc >= 0.999:
-                    chosen.add(c)
-                    acc -= 1.0
-            return chosen
+        half = TB // 2
 
-        vec_x, vec_y, accum = share(VEC_X), share(VEC_Y), share(ACCUM)
+        def z_half(c, n):
+            cols = slice(n * half, (n + 1) * half)
+            if n == 0:
+                zx[c] = psum.tile([P, TB], F32, name="zx", tag="zx", bufs=2)
+                zy[c] = psum.tile([P, TB], F32, name="zy", tag="zy", bufs=2)
+            for part, z in ((0, zx[c]), (1, zy[c])):
+                nc.tensor.matmul_mx(
+                    out=z[:, cols],
+                    lhsT=trig[part, 0][:, c * P : (c + 1) * P].bitcast(FP8X4),
+                    lhsT_scale=trig_plane[:, 0, part * F + c * P : part * F + (c + 1) * P],
+                    rhs=a_codes[0][:, cols].bitcast(FP8X4),
+                    rhs_scale=a_scales[0][:, cols],
+                    start=True,
+                    stop=True,
+                )
+
+        def square_half(c, n):
+            cols = slice(n * half, (n + 1) * half)
+            if n == 0:
+                xsq[c] = work.tile([P, TB], F32, name="xsq")
+                ysq[c] = work.tile([P, TB], F32, name="ysq", bufs=YB)
+            nc.scalar.activation(out=xsq[c][:, cols], in_=zx[c][:, cols], func=ACT.Square)
+            nc.scalar.activation(out=ysq[c][:, cols], in_=zy[c][:, cols], func=ACT.Square)
+
+        def share(slots):
+            first = 0 if slots is ACCUM else HALVED
+            return {c for c in range(first, CELLS) if c % 8 in slots[phase_of(c)]}
+
+        gps_y = share(GPS_Y)
+        vec_y = share(VEC_Y) - gps_y
+        vec_x, accum = share(VEC_X), share(ACCUM)
 
         def square_scalar(c):
+            if c < HALVED:
+                return
             if c not in vec_x:
                 xsq[c] = work.tile([P, TB], F32, name="xsq")
                 nc.scalar.activation(out=xsq[c][:], in_=zx[c][:], func=ACT.Square)
-            if c not in vec_y:
+            if c not in vec_y and c not in gps_y:
                 ysq[c] = work.tile([P, TB], F32, name="ysq", bufs=YB)
                 nc.scalar.activation(out=ysq[c][:], in_=zy[c][:], func=ACT.Square)
 
@@ -197,6 +235,13 @@ def tile_floored_inverse_filter_envelope_s4_kernel(
                         axis=AX.X,
                         op=ALU.mult,
                     )
+
+        def square_gpsimd(c):
+            if c in gps_y:
+                ycopy = work.tile([P, TB], F32, name="ycopy", bufs=2)
+                nc.vector.tensor_copy(out=ycopy[:], in_=zy[c][:])
+                ysq[c] = work.tile([P, TB], F32, name="ysq", bufs=YB)
+                nc.gpsimd.tensor_tensor(out=ysq[c][:], in0=ycopy[:], in1=ycopy[:], op=ALU.mult)
 
         def add_noise(c):
             i = c % 8
@@ -220,15 +265,15 @@ def tile_floored_inverse_filter_envelope_s4_kernel(
                     op1=ALU.add,
                 )
 
-        def transpose(q):
+        def transpose(q, tag="turn"):
             u, r = divmod(q, 4)
-            pt[u, r] = psum.tile([P, 4, P], F32, name="pt", tag="turn", bufs=4)
+            pt[q] = psum.tile([P, 4, P], F32, name="pt", tag=tag, bufs=4 if tag == "turn" else 2)
             for k in range(4):
                 c = 4 * u + k
                 parts = (power[c], ysq[c]) if c in accum else (power[c],)
                 for n, part in enumerate(parts):
                     nc.tensor.matmul(
-                        out=pt[u, r][:, k, :],
+                        out=pt[q][:, k, :],
                         lhsT=part[:, r * P : (r + 1) * P],
                         rhs=ident[:],
                         start=(n == 0),
@@ -236,52 +281,56 @@ def tile_floored_inverse_filter_envelope_s4_kernel(
                         is_transpose=True,
                     )
 
-        def take_log(u, r):
+        def place(q):
+            u, r = divmod(q, 4)
             b, h = divmod(u, 2)
             t = 4 * b + r
-            if t not in logp:
-                logp[t] = work.tile([P, F], F32, name="logp", bufs=10)
-            nc.scalar.activation(
-                out=logp[t][:, h * 512 : (h + 1) * 512],
-                in_=pt[u, r][:].rearrange("p k f -> p (k f)"),
-                func=ACT.Ln,
-            )
-            if h == 1:
-                neg = work.tile([P, F], F32, name="neg")
-                nc.gpsimd.tensor_scalar(
-                    out=neg[:], in0=logp[t][:], scalar1=-1.0, scalar2=0.0, op0=ALU.mult, op1=ALU.add
-                )
-                nc.sync.dma_start(out=log_out[t * P : (t + 1) * P, :], in_=neg[:])
+            return slice(t * P, (t + 1) * P), slice(h * 512, (h + 1) * 512)
 
-        def take_exp(t):
-            env = work.tile([P, F], F32, name="env", bufs=4)
-            nc.scalar.activation(out=env[:], in_=logp[t][:], func=ACT.Exp, scale=-1.0)
-            nc.sync.dma_start(out=env_out[t * P : (t + 1) * P, :], in_=env[:])
+        def take_log(q, engine=None):
+            rows, cols = place(q)
+            logp[q] = work.tile([P, 512], F32, name="logp", bufs=LB)
+            nc.scalar.activation(out=logp[q][:], in_=pt[q][:].rearrange("p k f -> p (k f)"), func=ACT.Ln)
+            neg = work.tile([P, 512], F32, name="neg", bufs=NB)
+            (engine or nc.gpsimd).tensor_scalar(out=neg[:], in0=logp[q][:], scalar1=-1.0, scalar2=0.0, op0=ALU.mult, op1=ALU.add)
+            nc.sync.dma_start(out=log_out[rows, cols], in_=neg[:])
+
+        def take_exp(q):
+            rows, cols = place(q)
+            env = work.tile([P, 512], F32, name="env", bufs=EB)
+            nc.scalar.activation(out=env[:], in_=logp[q][:], func=ACT.Exp, scale=-1.0)
+            nc.sync.dma_start(out=env_out[rows, cols], in_=env[:])
 
         for s in range(4):
             stage1_mm(s)
-            add_mean(s)
-            if s > 0:
-                quantise(s - 1)
-        quantise(3)
+        for n in range(2):
+            for s in (2 * n, 2 * n + 1):
+                add_mean(s)
+            for s in (2 * n, 2 * n + 1):
+                quantise(s)
+            for c in range(HALVED):
+                z_half(c, n)
+            for c in range(HALVED):
+                square_half(c, n)
         nc.vector.tensor_copy(out=noise_col[:], in_=noise_bf[:])
-        z_mm(0)
+        if HALVED == 0:
+            z_mm(0)
 
         turned = []
         q_next = 0
         logged, exped = set(), set()
 
-        def log_one():
+        def log_one(engine=None):
             q = turned.pop(0)
-            take_log(q // 4, q % 4)
+            take_log(q, engine)
             logged.add(q)
 
-        def exp_one(t):
-            take_exp(t)
-            exped.add(t)
+        def exp_one(q):
+            take_exp(q)
+            exped.add(q)
 
-        def ready_tiles():
-            return [t for t in range(16) if t not in exped and {8 * (t // 4) + t % 4, 8 * (t // 4) + 4 + t % 4} <= logged]
+        def ready():
+            return sorted(logged - exped)
 
         last_phase = "L"
         exps = []
@@ -290,21 +339,22 @@ def tile_floored_inverse_filter_envelope_s4_kernel(
             phase = phase_of(c)
             end = [c0 for c0, k in PHASES if c0 > c] + [CELLS]
             if phase == "E" and last_phase == "L":
-                exps = ready_tiles()
+                exps = ready()
             last_phase = phase
-            if c + 1 < CELLS:
+            if HALVED <= c + 1 < CELLS:
                 z_mm(c + 1)
-            s = 4 * (b + 1) + {0: 0, 1: 1, 3: 2, 4: 3}.get(i, 99)
+            s = 4 * (b + 1) + (S1.index(i) if i in S1 else 99)
             if s < 16:
                 stage1_mm(s)
             square_scalar(c)
             if c > 0:
                 add_noise(c - 1)
+            square_gpsimd(c)
             square_vector(c)
-            s1 = 4 * (b + 1) + {1: 0, 2: 1, 4: 2, 5: 3}.get(i, 99)
+            s1 = 4 * (b + 1) + (S1.index(i - DLY[0]) if i - DLY[0] in S1 else 99)
             if s1 < 16:
                 add_mean(s1)
-            s2 = 4 * (b + 1) + {2: 0, 3: 1, 5: 2, 6: 3}.get(i, 99)
+            s2 = 4 * (b + 1) + (S1.index(i - DLY[1]) if i - DLY[1] in S1 else 99)
             if s2 < 16:
                 quantise(s2)
             if phase == "L":
@@ -325,13 +375,24 @@ def tile_floored_inverse_filter_envelope_s4_kernel(
         add_noise(CELLS - 1)
         while turned:
             log_one()
-        rest = [8 * b + 4 * h + r for b in range(4) for r in range(4) for h in (0, 1)]
-        rest = [q for q in rest if q not in logged]
+        rest = [q for q in range(4 * CELLS // 4) if q not in logged]
+        inverse = []
         for n in range(len(rest) + 1):
             if n < len(rest):
-                transpose(rest[n])
+                transpose(rest[n], "turn" if n >= RECIP else ("zx", "zy")[n % 2])
                 turned.append(rest[n])
             if n > 0:
-                log_one()
-        for t in ready_tiles():
-            exp_one(t)
+                q = rest[n - 1]
+                log_one(nc.vector if TAILNEG else nc.gpsimd)
+                if n <= RECIP:
+                    inv = work.tile([P, 512], F32, name="inverse", bufs=4)
+                    nc.vector.reciprocal(out=inv[:], in_=pt[q][:].rearrange("p k f -> p (k f)"))
+                    inverse.append((q, inv))
+                    exped.add(q)
+        last = ready()
+        for n, q in enumerate(last):
+            exp_one(q)
+            if inverse and n >= len(last) - 2 - len(inverse):
+                q, inv = inverse.pop(0)
+                rows, cols = place(q)
+                nc.sync.dma_start(out=env_out[rows, cols], in_=inv[:])

@@ -20,24 +20,25 @@ AX = mybir.AxisListType
 G = M // 512
 TB = 512
 CELLS = (T // TB) * (F // P)
-PHASES = ((0, "L"),)
-VEC_Y = {"L": (0, 1, 3, 6), "E": ()}
-GPS_Y = {"L": (), "E": ()}
-VEC_X = {"L": (), "E": ()}
-ACCUM = {"L": (0, 2), "E": ()}
+PHASES = ((0, "L"), (24, "E"))
+VEC_Y = {"L": (1, 3, 7), "E": (0, 1, 3, 4, 6, 7)}
+GPS_Y = {"L": (), "E": (0, 1, 2, 4, 5)}
+VEC_X = {"L": (), "E": (0, 1, 2, 4, 5, 6, 7)}
+ACCUM = {"L": (1, 2), "E": (0, 1, 2, 3, 4, 5, 6)}
 TURNS = 2
 LOGS = 2
-LAG = 5
+LAG = 6
 RECIP = 0
+WARM = 28
 TAILNEG = 1
 PLANE_V = 4
 HALVED = 2
-S1 = (0, 2, 3, 4)
+S1 = (0, 1, 3, 4)
 DLY = (1, 2)
-YB = 18
-PB = 10
-LB = 32
-EB = 8
+YB = 14
+PB = 14
+LB = 16
+EB = 5
 NB = 6
 
 
@@ -83,34 +84,40 @@ def tile_floored_inverse_filter_envelope_s4_kernel(
                 in_=source.bitcast(I32)[:, 4 * q : 4 * q + 4, :].rearrange("g r n -> r g n"),
             )
 
-        for q in range(4):
-            load_scales(nc.scalar, book_plane, book_scales, q)
+        load_scales(nc.scalar, book_plane, book_scales, 0)
+        load_scales(nc.scalar, book_plane, book_scales, 1)
+        load_scales(nc.sync, book_plane, book_scales, 2)
+        load_scales(nc.sync, book_plane, book_scales, 3)
         load_codes(0)
         load_scales(nc.scalar, code_plane, code_scales, 0)
-        load_scales(nc.scalar, code_plane, code_scales, 1)
-        load_scales(nc.gpsimd, code_plane, code_scales, 2)
-        load_scales(nc.gpsimd, code_plane, code_scales, 3)
+        load_scales(nc.sync, code_plane, code_scales, 1)
+        load_scales(nc.scalar, code_plane, code_scales, 2)
+        load_scales(nc.sync, code_plane, code_scales, 3)
         mean_col = const.tile([P, 4], BF16, name="mean_col")
         nc.sync.dma_start(out=mean_col[:], in_=mean.rearrange("(p j) -> p j", j=4))
         for q in range(4):
             load_scales(nc.sync, trig_plane, trig_scales, q)
         load_trig(0, 0)
         load_trig(1, 0)
-        noise_bf = const.tile([P, F // P], BF16, name="noise_bf")
-        with nc.allow_non_contiguous_dma(reason="one noise value of each 128-frequency tile a partition"):
-            nc.sync.dma_start(out=noise_bf[:], in_=noise.rearrange("(i p) -> p i", p=P))
         load_codes(1)
         load_trig(0, 1)
         load_trig(1, 1)
         load_codes(2)
         load_codes(3)
 
-        one = const.tile([P, 1], F32, name="one")
-        nc.gpsimd.memset(one[:], 1.0)
-        warm = const.tile([P, 1], F32, name="warm")
-        nc.scalar.activation(out=warm[:], in_=one[:], func=ACT.Ln)
         ident = const.tile([P, P], F32, name="ident")
+        warm = const.tile([P, 1], F32, name="warm")
+        one = const.tile([P, 1], F32, name="one")
+        nc.vector.memset(one[:], 1.0)
+        nc.scalar.activation(out=warm[:], in_=one[:], func=ACT.Ln)
         make_identity(nc, ident[:])
+        if WARM:
+            spare = psum.tile([P, 4, P], F32, name="spare", tag="turn", bufs=4)
+            for n in range(WARM):
+                nc.tensor.transpose(spare[:, n % 4, :], ident[:], ident[:])
+        noise_bf = const.tile([P, F // P], BF16, name="noise_bf")
+        with nc.allow_non_contiguous_dma(reason="one noise value of each 128-frequency tile a partition"):
+            nc.gpsimd.dma_start(out=noise_bf[:], in_=noise.rearrange("(i p) -> p i", p=P))
 
         book_codes = [const.tile([P, G, 2 * P], U8, name="book_codes%d" % j, align_bytes=64) for j in range(4)]
         book_pp = [const.tile([P, G, P], U8, name="book_pp%d" % j, align_bytes=64) for j in range(4)]
@@ -289,17 +296,19 @@ def tile_floored_inverse_filter_envelope_s4_kernel(
 
         def take_log(q, engine=None):
             rows, cols = place(q)
-            logp[q] = work.tile([P, 512], F32, name="logp", bufs=LB)
-            nc.scalar.activation(out=logp[q][:], in_=pt[q][:].rearrange("p k f -> p (k f)"), func=ACT.Ln)
+            t = rows.start // P
+            if t not in logp:
+                logp[t] = work.tile([P, F], F32, name="logp", bufs=LB)
+            nc.scalar.activation(out=logp[t][:, cols], in_=pt[q][:].rearrange("p k f -> p (k f)"), func=ACT.Ln)
             neg = work.tile([P, 512], F32, name="neg", bufs=NB)
-            (engine or nc.gpsimd).tensor_scalar(out=neg[:], in0=logp[q][:], scalar1=-1.0, scalar2=0.0, op0=ALU.mult, op1=ALU.add)
+            (engine or nc.gpsimd).tensor_scalar(out=neg[:], in0=logp[t][:, cols], scalar1=-1.0, scalar2=0.0, op0=ALU.mult, op1=ALU.add)
             nc.sync.dma_start(out=log_out[rows, cols], in_=neg[:])
 
-        def take_exp(q):
-            rows, cols = place(q)
-            env = work.tile([P, 512], F32, name="env", bufs=EB)
-            nc.scalar.activation(out=env[:], in_=logp[q][:], func=ACT.Exp, scale=-1.0)
-            nc.sync.dma_start(out=env_out[rows, cols], in_=env[:])
+        def take_exp(t, cols):
+            w = cols.stop - cols.start
+            env = work.tile([P, F], F32, name="env", bufs=EB)
+            nc.scalar.activation(out=env[:, :w], in_=logp[t][:, cols], func=ACT.Exp, scale=-1.0)
+            nc.sync.dma_start(out=env_out[t * P : (t + 1) * P, cols], in_=env[:, :w])
 
         for s in range(4):
             stage1_mm(s)
@@ -325,12 +334,17 @@ def tile_floored_inverse_filter_envelope_s4_kernel(
             take_log(q, engine)
             logged.add(q)
 
-        def exp_one(q):
-            take_exp(q)
-            exped.add(q)
+        def exp_one(job):
+            t, halves = job
+            take_exp(t, slice(halves[0] * 512, (halves[-1] + 1) * 512))
+            exped.update(8 * (t // 4) + 4 * h + t % 4 for h in halves)
 
         def ready():
-            return sorted(logged - exped)
+            jobs = {}
+            for q in sorted(logged - exped):
+                t = 4 * (q // 8) + q % 4
+                jobs.setdefault(t, []).append(q // 4 % 2)
+            return [(t, jobs[t]) for t in sorted(jobs)]
 
         last_phase = "L"
         exps = []
@@ -390,8 +404,11 @@ def tile_floored_inverse_filter_envelope_s4_kernel(
                     inverse.append((q, inv))
                     exped.add(q)
         last = ready()
-        for n, q in enumerate(last):
-            exp_one(q)
+        for n, job in enumerate(last):
+            if n == len(last) - 1 and len(job[1]) == 2:
+                exp_one((job[0], job[1][:1]))
+                job = (job[0], job[1][1:])
+            exp_one(job)
             if inverse and n >= len(last) - 2 - len(inverse):
                 q, inv = inverse.pop(0)
                 rows, cols = place(q)

from contextlib import ExitStack

import concourse.mybir as mybir
from concourse.masks import make_identity

T, M, L, F = 2048, 1024, 512, 1024
P = 128
FLOPS = 2 * T * M * L + 2 * T * L * 2 * F + 6 * T * F
F32 = mybir.dt.float32
BF16 = mybir.dt.bfloat16
I32 = mybir.dt.int32
U32 = mybir.dt.uint32
U8 = mybir.dt.uint8
FP4X4 = mybir.dt.float4_e2m1fn_x4
FP8X4 = mybir.dt.float8_e4m3fn_x4
ACT = mybir.ActivationFunctionType
ALU = mybir.AluOpType
AX = mybir.AxisListType

G = M // 512
TB = 512
CELLS = (T // TB) * (F // P)
PHASES = ((0, "L"), (24, "E"))
VEC_Y = {"L": (1, 3, 7), "E": (0, 1, 3, 4, 6, 7)}
GPS_Y = {"L": (), "E": (0, 1, 2, 4, 5)}
VEC_X = {"L": (), "E": (0, 1, 2, 4, 5, 6, 7)}
ACCUM = {"L": (1, 2), "E": (0, 1, 2, 3, 4, 5, 6)}
TURNS = 2
LOGS = 2
LAG = 6
RECIP = 0
WARM = 28
TAILNEG = 1
PLANE_V = 4
HALVED = 2
S1 = (0, 1, 3, 4)
DLY = (1, 2)
YB = 14
PB = 14
LB = 16
EB = 5
NB = 6


def tile_floored_inverse_filter_envelope_s4_kernel(
    tc, code_words, code_scales, book_words, book_scales, mean, trig_words, trig_scales, noise, env_out, log_out
):
    nc = tc.nc
    with ExitStack() as ctx:
        const = ctx.enter_context(tc.tile_pool(name="const", bufs=1))
        work = ctx.enter_context(tc.tile_pool(name="work", bufs=3))
        psum = ctx.enter_context(tc.psum_pool(name="psum", bufs=2))
        ctx.enter_context(tc.manual_schedule())

        book_plane = const.tile([P, G, L], U8, name="book_plane", align_bytes=64)
        code_plane = const.tile([P, G, T], U8, name="code_plane", align_bytes=64)
        trig_plane = const.tile([P, 1, 2 * F], U8, name="trig_plane", align_bytes=64)
        for plane in (book_plane, code_plane, trig_plane):
            nc.vector.memset(plane[:].rearrange("p g n -> p (g n)").bitcast(I32), 0)
        book_raw = const.tile([P, G, 2 * L], U8, name="book_raw", align_bytes=64)
        nc.sync.dma_start(out=book_raw[:].bitcast(I32), in_=book_words.bitcast(I32).rearrange("g p n -> p g n"))
        code_tiles = []
        for b in range(T // TB):
            code_tiles.append(const.tile([P, G, 2 * TB], U8, name="codes%d" % b, align_bytes=64))
        cw = code_words.bitcast(I32).rearrange("g p n -> p g n")
        w32 = 2 * TB // 4

        def load_codes(b):
            nc.sync.dma_start(out=code_tiles[b][:].bitcast(I32), in_=cw[:, :, b * w32 : (b + 1) * w32])

        trig = {}
        tw = trig_words.rearrange("g p n t -> p (g n t)").bitcast(I32)
        for part in (0, 1):
            for h in (0, 1):
                trig[part, h] = const.tile([P, 512], I32, name="trig%d%d" % (part, h), align_bytes=64)

        def load_trig(part, h):
            n0 = part * F + h * 512
            nc.sync.dma_start(out=trig[part, h][:], in_=tw[:, n0 : n0 + 512])

        def load_scales(queue, plane, source, q):
            queue.dma_start(
                out=plane[:].bitcast(I32)[32 * q : 32 * q + 4],
                in_=source.bitcast(I32)[:, 4 * q : 4 * q + 4, :].rearrange("g r n -> r g n"),
            )

        load_scales(nc.scalar, book_plane, book_scales, 0)
        load_scales(nc.scalar, book_plane, book_scales, 1)
        load_scales(nc.sync, book_plane, book_scales, 2)
        load_scales(nc.sync, book_plane, book_scales, 3)
        load_codes(0)
        load_scales(nc.scalar, code_plane, code_scales, 0)
        load_scales(nc.sync, code_plane, code_scales, 1)
        load_scales(nc.scalar, code_plane, code_scales, 2)
        load_scales(nc.sync, code_plane, code_scales, 3)
        mean_col = const.tile([P, 4], BF16, name="mean_col")
        nc.sync.dma_start(out=mean_col[:], in_=mean.rearrange("(p j) -> p j", j=4))
        for q in range(4):
            load_scales(nc.sync, trig_plane, trig_scales, q)
        load_trig(0, 0)
        load_trig(1, 0)
        load_codes(1)
        load_trig(0, 1)
        load_trig(1, 1)
        load_codes(2)
        load_codes(3)

        ident = const.tile([P, P], F32, name="ident")
        warm = const.tile([P, 1], F32, name="warm")
        one = const.tile([P, 1], F32, name="one")
        nc.vector.memset(one[:], 1.0)
        nc.scalar.activation(out=warm[:], in_=one[:], func=ACT.Ln)
        make_identity(nc, ident[:])
        if WARM:
            spare = psum.tile([P, 4, P], F32, name="spare", tag="turn", bufs=4)
            for n in range(WARM):
                nc.tensor.transpose(spare[:, n % 4, :], ident[:], ident[:])
        noise_bf = const.tile([P, F // P], BF16, name="noise_bf")
        with nc.allow_non_contiguous_dma(reason="one noise value of each 128-frequency tile a partition"):
            nc.gpsimd.dma_start(out=noise_bf[:], in_=noise.rearrange("(i p) -> p i", p=P))

        book_codes = [const.tile([P, G, 2 * P], U8, name="book_codes%d" % j, align_bytes=64) for j in range(4)]
        book_pp = [const.tile([P, G, P], U8, name="book_pp%d" % j, align_bytes=64) for j in range(4)]
        raw_by_slot = book_raw[:].rearrange("p g (m j b) -> p g j m b", j=4, b=2)
        plane_by_slot = book_plane[:].rearrange("p g (m j) -> p g j m", j=4)
        for j in range(4):
            nc.vector.tensor_copy(
                out=book_codes[j][:].rearrange("p g (m b) -> p g m b", b=2), in_=raw_by_slot[:, :, j]
            )
            engine = nc.vector if j < PLANE_V else nc.gpsimd
            engine.tensor_copy(out=book_pp[j][:], in_=plane_by_slot[:, :, j])
        noise_col = const.tile([P, F // P], F32, name="noise_col")

        a_ps, a_bf, a_codes, a_scales, zx, zy, xsq, ysq, power, pt, logp = ({} for _ in range(11))

        def stage1_mm(s):
            b, r = divmod(s, 4)
            a_ps[s] = psum.tile([P, 4, P], F32, name="a_ps", tag="turn", bufs=4)
            for j in range(4):
                for g in range(G):
                    nc.tensor.matmul_mx(
                        out=a_ps[s][:, j, :],
                        lhsT=book_codes[j][:, g, :].bitcast(FP4X4),
                        lhsT_scale=book_pp[j][:, g, :],
                        rhs=code_tiles[b][:, g, 2 * P * r : 2 * P * (r + 1)].bitcast(FP4X4),
                        rhs_scale=code_plane[:, g, s * P : (s + 1) * P],
                        start=(g == 0),
                        stop=(g == G - 1),
                    )

        def add_mean(s):
            a_bf[s] = work.tile([P, P, 4], BF16, name="a_bf", align_bytes=64)
            nc.vector.tensor_tensor(
                out=a_bf[s][:],
                in0=a_ps[s][:].rearrange("p j n -> p n j"),
                in1=mean_col[:].unsqueeze(1).to_broadcast([P, P, 4]),
                op=ALU.add,
            )

        def quantise(s):
            b, r = divmod(s, 4)
            if r == 0:
                a_codes[b] = work.tile([P, TB], U32, name="a_codes", align_bytes=64, bufs=2)
                a_scales[b] = work.tile([P, TB], U8, name="a_scales", align_bytes=64, bufs=2)
            cols = slice(r * P, (r + 1) * P)
            nc.vector.quantize_mx(
                out=a_codes[b][:, cols].bitcast(FP8X4),
                scales=a_scales[b][:, cols],
                in_=a_bf[s][:].rearrange("p n j -> p (n j)"),
            )

        def z_mm(c):
            b, i = divmod(c, 8)
            h, k = divmod(i, 4)
            zx[c] = psum.tile([P, TB], F32, name="zx", tag="zx", bufs=2)
            zy[c] = psum.tile([P, TB], F32, name="zy", tag="zy", bufs=2)
            for part, z in ((0, zx[c]), (1, zy[c])):
                nc.tensor.matmul_mx(
                    out=z[:],
                    lhsT=trig[part, h][:, k * P : (k + 1) * P].bitcast(FP8X4),
                    lhsT_scale=trig_plane[:, 0, part * F + i * P : part * F + (i + 1) * P],
                    rhs=a_codes[b][:].bitcast(FP8X4),
                    rhs_scale=a_scales[b][:],
                    start=True,
                    stop=True,
                )

        def phase_of(c):
            return [k for c0, k in PHASES if c0 <= c][-1]

        half = TB // 2

        def z_half(c, n):
            cols = slice(n * half, (n + 1) * half)
            if n == 0:
                zx[c] = psum.tile([P, TB], F32, name="zx", tag="zx", bufs=2)
                zy[c] = psum.tile([P, TB], F32, name="zy", tag="zy", bufs=2)
            for part, z in ((0, zx[c]), (1, zy[c])):
                nc.tensor.matmul_mx(
                    out=z[:, cols],
                    lhsT=trig[part, 0][:, c * P : (c + 1) * P].bitcast(FP8X4),
                    lhsT_scale=trig_plane[:, 0, part * F + c * P : part * F + (c + 1) * P],
                    rhs=a_codes[0][:, cols].bitcast(FP8X4),
                    rhs_scale=a_scales[0][:, cols],
                    start=True,
                    stop=True,
                )

        def square_half(c, n):
            cols = slice(n * half, (n + 1) * half)
            if n == 0:
                xsq[c] = work.tile([P, TB], F32, name="xsq")
                ysq[c] = work.tile([P, TB], F32, name="ysq", bufs=YB)
            nc.scalar.activation(out=xsq[c][:, cols], in_=zx[c][:, cols], func=ACT.Square)
            nc.scalar.activation(out=ysq[c][:, cols], in_=zy[c][:, cols], func=ACT.Square)

        def share(slots):
            first = 0 if slots is ACCUM else HALVED
            return {c for c in range(first, CELLS) if c % 8 in slots[phase_of(c)]}

        gps_y = share(GPS_Y)
        vec_y = share(VEC_Y) - gps_y
        vec_x, accum = share(VEC_X), share(ACCUM)

        def square_scalar(c):
            if c < HALVED:
                return
            if c not in vec_x:
                xsq[c] = work.tile([P, TB], F32, name="xsq")
                nc.scalar.activation(out=xsq[c][:], in_=zx[c][:], func=ACT.Square)
            if c not in vec_y and c not in gps_y:
                ysq[c] = work.tile([P, TB], F32, name="ysq", bufs=YB)
                nc.scalar.activation(out=ysq[c][:], in_=zy[c][:], func=ACT.Square)

        def square_vector(c):
            for chosen, z, sq, tag in ((vec_x, zx, xsq, "xsq"), (vec_y, zy, ysq, "ysq")):
                if c in chosen:
                    sq[c] = work.tile([P, TB], F32, name=tag, bufs=YB if tag == "ysq" else 3)
                    nc.vector.tensor_reduce(
                        out=sq[c][:],
                        in_=z[c][:].unsqueeze(2).to_broadcast([P, TB, 2]),
                        axis=AX.X,
                        op=ALU.mult,
                    )

        def square_gpsimd(c):
            if c in gps_y:
                ycopy = work.tile([P, TB], F32, name="ycopy", bufs=2)
                nc.vector.tensor_copy(out=ycopy[:], in_=zy[c][:])
                ysq[c] = work.tile([P, TB], F32, name="ysq", bufs=YB)
                nc.gpsimd.tensor_tensor(out=ysq[c][:], in0=ycopy[:], in1=ycopy[:], op=ALU.mult)

        def add_noise(c):
            i = c % 8
            power[c] = work.tile([P, TB], F32, name="power", bufs=PB)
            if c in accum:
                nc.gpsimd.tensor_scalar(
                    out=power[c][:],
                    in0=xsq[c][:],
                    scalar1=1.0,
                    scalar2=noise_col[:, i : i + 1],
                    op0=ALU.mult,
                    op1=ALU.add,
                )
            else:
                nc.vector.scalar_tensor_tensor(
                    out=power[c][:],
                    in0=xsq[c][:],
                    scalar=noise_col[:, i : i + 1],
                    in1=ysq[c][:],
                    op0=ALU.add,
                    op1=ALU.add,
                )

        def transpose(q, tag="turn"):
            u, r = divmod(q, 4)
            pt[q] = psum.tile([P, 4, P], F32, name="pt", tag=tag, bufs=4 if tag == "turn" else 2)
            for k in range(4):
                c = 4 * u + k
                parts = (power[c], ysq[c]) if c in accum else (power[c],)
                for n, part in enumerate(parts):
                    nc.tensor.matmul(
                        out=pt[q][:, k, :],
                        lhsT=part[:, r * P : (r + 1) * P],
                        rhs=ident[:],
                        start=(n == 0),
                        stop=(n == len(parts) - 1),
                        is_transpose=True,
                    )

        def place(q):
            u, r = divmod(q, 4)
            b, h = divmod(u, 2)
            t = 4 * b + r
            return slice(t * P, (t + 1) * P), slice(h * 512, (h + 1) * 512)

        def take_log(q, engine=None):
            rows, cols = place(q)
            t = rows.start // P
            if t not in logp:
                logp[t] = work.tile([P, F], F32, name="logp", bufs=LB)
            nc.scalar.activation(out=logp[t][:, cols], in_=pt[q][:].rearrange("p k f -> p (k f)"), func=ACT.Ln)
            neg = work.tile([P, 512], F32, name="neg", bufs=NB)
            (engine or nc.gpsimd).tensor_scalar(out=neg[:], in0=logp[t][:, cols], scalar1=-1.0, scalar2=0.0, op0=ALU.mult, op1=ALU.add)
            nc.sync.dma_start(out=log_out[rows, cols], in_=neg[:])

        def take_exp(t, cols):
            w = cols.stop - cols.start
            env = work.tile([P, F], F32, name="env", bufs=EB)
            nc.scalar.activation(out=env[:, :w], in_=logp[t][:, cols], func=ACT.Exp, scale=-1.0)
            nc.sync.dma_start(out=env_out[t * P : (t + 1) * P, cols], in_=env[:, :w])

        for s in range(4):
            stage1_mm(s)
        for n in range(2):
            for s in (2 * n, 2 * n + 1):
                add_mean(s)
            for s in (2 * n, 2 * n + 1):
                quantise(s)
            for c in range(HALVED):
                z_half(c, n)
            for c in range(HALVED):
                square_half(c, n)
        nc.vector.tensor_copy(out=noise_col[:], in_=noise_bf[:])
        if HALVED == 0:
            z_mm(0)

        turned = []
        q_next = 0
        logged, exped = set(), set()

        def log_one(engine=None):
            q = turned.pop(0)
            take_log(q, engine)
            logged.add(q)

        def exp_one(job):
            t, halves = job
            take_exp(t, slice(halves[0] * 512, (halves[-1] + 1) * 512))
            exped.update(8 * (t // 4) + 4 * h + t % 4 for h in halves)

        def ready():
            jobs = {}
            for q in sorted(logged - exped):
                t = 4 * (q // 8) + q % 4
                jobs.setdefault(t, []).append(q // 4 % 2)
            return [(t, jobs[t]) for t in sorted(jobs)]

        last_phase = "L"
        exps = []
        for c in range(CELLS):
            b, i = divmod(c, 8)
            phase = phase_of(c)
            end = [c0 for c0, k in PHASES if c0 > c] + [CELLS]
            if phase == "E" and last_phase == "L":
                exps = ready()
            last_phase = phase
            if HALVED <= c + 1 < CELLS:
                z_mm(c + 1)
            s = 4 * (b + 1) + (S1.index(i) if i in S1 else 99)
            if s < 16:
                stage1_mm(s)
            square_scalar(c)
            if c > 0:
                add_noise(c - 1)
            square_gpsimd(c)
            square_vector(c)
            s1 = 4 * (b + 1) + (S1.index(i - DLY[0]) if i - DLY[0] in S1 else 99)
            if s1 < 16:
                add_mean(s1)
            s2 = 4 * (b + 1) + (S1.index(i - DLY[1]) if i - DLY[1] in S1 else 99)
            if s2 < 16:
                quantise(s2)
            if phase == "L":
                n = min(len(turned), LOGS)
                for _ in range(n):
                    log_one()
            else:
                n = -(-len(exps) // (end[0] - c))
                for _ in range(n):
                    exp_one(exps.pop(0))
            ready_q = 4 * (((c - LAG) // 4) + 1) if c >= LAG else 0
            n = 0
            while n < max(TURNS, 1 if phase == "E" else (ready_q - q_next + 3) // 4) and len(turned) < 2 and q_next < ready_q:
                transpose(q_next)
                turned.append(q_next)
                q_next += 1
                n += 1
        add_noise(CELLS - 1)
        while turned:
            log_one()
        rest = [q for q in range(4 * CELLS // 4) if q not in logged]
        inverse = []
        for n in range(len(rest) + 1):
            if n < len(rest):
                transpose(rest[n], "turn" if n >= RECIP else ("zx", "zy")[n % 2])
                turned.append(rest[n])
            if n > 0:
                q = rest[n - 1]
                log_one(nc.vector if TAILNEG else nc.gpsimd)
                if n <= RECIP:
                    inv = work.tile([P, 512], F32, name="inverse", bufs=4)
                    nc.vector.reciprocal(out=inv[:], in_=pt[q][:].rearrange("p k f -> p (k f)"))
                    inverse.append((q, inv))
                    exped.add(q)
        last = ready()
        for n, job in enumerate(last):
            if n == len(last) - 1 and len(job[1]) == 2:
                exp_one((job[0], job[1][:1]))
                job = (job[0], job[1][1:])
            exp_one(job)
            if inverse and n >= len(last) - 2 - len(inverse):
                q, inv = inverse.pop(0)
                rows, cols = place(q)
                nc.sync.dma_start(out=env_out[rows, cols], in_=inv[:])
